import numpy as np
import ml_dtypes


def mxq(x, axis, fmt="e4m3"):
    dtype, down = {"e4m3": (ml_dtypes.float8_e4m3fn, 7), "e5m2": (ml_dtypes.float8_e5m2, 14)}[fmt]
    v = np.moveaxis(np.asarray(x, np.float32).astype(ml_dtypes.bfloat16).astype(np.float64), axis, -1)
    blocks = v.reshape(v.shape[:-1] + (-1, 32))
    amax = np.abs(blocks).max(-1, keepdims=True)
    byte = np.maximum(np.where(amax > 0, np.frexp(amax)[1] - 1 + 127, 0) - down, 1)
    scale = np.exp2(byte - 127.0)
    codes = (blocks / scale).astype(np.float32).astype(dtype).astype(np.float64)
    return np.moveaxis((codes * scale).reshape(v.shape), -1, axis)


WIDE = False


def mx_kscale(k):
    if not WIDE:
        return np.ones(k)
    levels = np.array([10, -10, 5, -5, 0])
    if k % 512:
        return np.exp2(np.random.permutation(np.resize(levels, k // 32))).repeat(32)
    a = np.empty((k // 512, 16))
    for p in range(k // 512):
        a[p, :8] = np.random.permutation(np.resize(levels, 8))
        for g in range(8):
            far = levels[np.abs(levels - a[p, g]) >= 10]
            a[p, g + 8] = far[np.random.randint(len(far))]
    return np.exp2(a.ravel()).repeat(32)


def f64(x):
    return np.asarray(x).astype(np.float64)


def striped(idx):
    return np.tile(idx.reshape(-1, 16).T, (8, 1)).astype(np.uint16)


def unstriped(offs):
    return offs[:16].T.reshape(-1).astype(np.int64)


E2M1 = np.array([0.0, 0.5, 1.0, 1.5, 2.0, 3.0, 4.0, 6.0, -0.0, -0.5, -1.0, -1.5, -2.0, -3.0, -4.0, -6.0])


def pack_weight(w, fmt):
    k, n = w.shape
    w = f64(np.asarray(w, np.float32).astype(ml_dtypes.bfloat16)).reshape(k // 32, 32, n)
    amax = np.abs(w).max(1)
    if fmt == "e4m3":
        byte = np.frexp(amax)[1] - 1 + 127 - 7
    else:
        mant, ex = np.frexp(amax / 6.0)
        byte = np.where(mant > 0.5, ex, ex - 1) + 127
    byte = np.clip(np.where(amax > 0, byte, 1), 1, 254)
    scaled = (w * np.exp2(127.0 - byte)[:, None, :]).reshape(k, n).astype(np.float32)
    by_word = np.ascontiguousarray(scaled.reshape(k // 512, 128, 4, n).transpose(0, 1, 3, 2))
    if fmt == "e4m3":
        words = by_word.astype(ml_dtypes.float8_e4m3fn).view(np.uint8)
    else:
        c = by_word.astype(ml_dtypes.float4_e2m1fn).view(np.uint8) & 0xF
        words = (c[..., 0::2] | (c[..., 1::2] << 4)).reshape(k // 512, 128, 2 * n)
    return np.ascontiguousarray(words), np.ascontiguousarray(byte.astype(np.uint8).reshape(k // 512, 16, n))


def unpack_weight(words, scales, fmt):
    g, _, n = scales.shape
    words = np.ascontiguousarray(words).reshape(g, 128, n, -1)
    if fmt == "e4m3":
        vals = words.view(ml_dtypes.float8_e4m3fn).astype(np.float64)
    else:
        nib = np.empty((g, 128, n, 4), np.uint8)
        nib[..., 0::2] = words & 0xF
        nib[..., 1::2] = words >> 4
        vals = E2M1[nib]
    vals = vals * np.repeat(np.exp2(scales.astype(np.float64) - 127.0), 8, axis=1)[..., None]
    return vals.transpose(0, 1, 3, 2).reshape(g * 512, n)


def pack_table(v):
    words, scales = pack_weight(v, "e4m3")
    return np.concatenate([words.reshape(words.shape[0], -1), scales.reshape(scales.shape[0], -1)], axis=1)


def unpack_table(tab):
    g, t = tab.shape[0], tab.shape[1] // 528
    return unpack_weight(tab[:, :512 * t].reshape(g, 128, t, 4), tab[:, 512 * t:].reshape(g, 16, t), "e4m3")


def silu(v):
    return v / (1.0 + np.exp(-np.maximum(v, -700.0)))


K, L, M, T, S = 1024, 1536, 256, 4096, 1536


def setup_inputs():
    n = np.random.standard_normal
    s1 = mx_kscale(K)[:, None]
    s2 = mx_kscale(L)[:, None]
    p_w4 = pack_weight(n((K, M)) / np.sqrt(K) / s1, "e2m1")
    return {
        "tab": pack_table(n((K, T)) * s1),
        "w4_words": p_w4[0],
        "w4_scales": p_w4[1],
        "x": (n((L, S)) * s2).astype(np.float32),
        "u": (n((L, M)) / np.sqrt(L) / s2).astype(np.float32),
        "b": (0.3 * n(256)).astype(np.float32),
        "offs": striped(np.random.permutation(T)[:S]),
    }


def reference(tab, w4_words, w4_scales, x, u, b, offs):
    tab_ = unpack_table(tab)[:, unstriped(offs)]
    w4_ = unpack_weight(w4_words, w4_scales, "e2m1")
    x_ = mxq(f64(x), 0, "e4m3")
    u_ = mxq(f64(u), 0, "e4m3")
    y = w4_.T @ tab_ + u_.T @ x_
    return silu(y + f64(b)[:, None])

@@ -1,0 +1,188 @@
+from contextlib import ExitStack
+
+import concourse.mybir as mybir
+
+K, L, M, T, S = 1024, 1536, 256, 4096, 1536
+FLOPS = 2 * M * S * (K + L)
+
+F32 = mybir.dt.float32
+BF16 = mybir.dt.bfloat16
+I32 = mybir.dt.int32
+U32 = mybir.dt.uint32
+U16 = mybir.dt.uint16
+U8 = mybir.dt.uint8
+E4M3 = mybir.dt.float8_e4m3fn_x4
+E2M1 = mybir.dt.float4_e2m1fn_x4
+SILU = mybir.ActivationFunctionType.Silu
+
+P = 128
+PACK = 4
+K_PASS = P * PACK
+W_PASSES = K // K_PASS
+U_PASSES = L // K_PASS
+HALVES = M // P
+WORD_BYTES = K_PASS * T
+SCALE_ROWS = 16
+
+GROUPS = ((0, 512), (512, 512), (1024, 512))
+
+
+def tile_list_tabx_silu_kernel(tc, tab, w4_words, w4_scales, x, u, b, offs, out):
+    nc = tc.nc
+    with ExitStack() as ctx:
+        keep = ctx.enter_context(tc.tile_pool(name="keep", bufs=1))
+        psum = ctx.enter_context(tc.psum_pool(name="psum", bufs=1))
+
+        offsets = keep.tile([P, S // 16], U16, name="offsets")
+        nc.sync.dma_start(offsets[:], offs)
+
+        act_in = keep.tile([P, 8], F32, name="act_in")
+        act_out = keep.tile([P, 8], F32, name="act_out")
+        nc.vector.memset(act_in[:], 0.0)
+        nc.scalar.activation(out=act_out[:], in_=act_in[:], func=SILU)
+
+        tab_scales = keep.tile([P, T], U8, name="tab_scales", align_bytes=64)
+        nc.vector.memset(tab_scales[:].bitcast(I32), 0)
+        w_scales = keep.tile([P, W_PASSES, M], U8, name="w_scales", align_bytes=64)
+        nc.vector.memset(w_scales[:].rearrange("p a n -> p (a n)").bitcast(I32), 0)
+        moved_scales = keep.tile([P, S], U8, name="moved_scales", align_bytes=64)
+        nc.vector.memset(moved_scales[:].bitcast(I32), 0)
+
+        u_raw = keep.tile([P, U_PASSES, PACK, M], F32, name="u_raw")
+        nc.sync.dma_start(
+            u_raw[:].rearrange("p a i n -> p a (i n)"), u.rearrange("(a p i) n -> p a (i n)", p=P, i=PACK)
+        )
+        x_raw = [keep.tile([P, PACK, S], F32, name="x_raw%d" % a) for a in range(U_PASSES)]
+        x_rows = x.rearrange("(a p i) j -> a p i j", p=P, i=PACK)
+        tab_words = [keep.tile([P, T], I32, name="tab_words%d" % a) for a in range(W_PASSES)]
+
+        def load_words(a):
+            nc.sync.dma_start(
+                tab_words[a][:], tab[a, 0:WORD_BYTES].rearrange("(p n) -> p n", p=P).bitcast(I32)
+            )
+
+        nc.sync.dma_start(x_raw[0][:], x_rows[0])
+        w_words = keep.tile([P, W_PASSES, 2 * M], U8, name="w_words", align_bytes=64)
+        nc.sync.dma_start(
+            w_words[:].bitcast(I32), w4_words.bitcast(I32).rearrange("a p n -> p a n")
+        )
+        scale_rows = tab[:, WORD_BYTES : WORD_BYTES + SCALE_ROWS * T].bitcast(I32)
+        rows0 = scale_rows[0].rearrange("(Q r t) -> r Q t", Q=4, r=4)
+        for r in range(4):
+            nc.sync.dma_start(tab_scales[r : P : 32, :].bitcast(I32), rows0[r])
+        nc.sync.dma_start(
+            tab_scales[4 : P : 8, :].bitcast(I32), scale_rows[1].rearrange("(q t) -> q t", q=SCALE_ROWS)
+        )
+        load_words(0)
+        nc.sync.dma_start(x_raw[1][:], x_rows[1])
+        ws = w4_scales.bitcast(I32).rearrange("a (Q r) n -> r Q a n", r=4)
+        for r in range(4):
+            nc.sync.dma_start(w_scales[r : P : 32, :, :].bitcast(I32), ws[r])
+        bias = keep.tile([P, HALVES], F32, name="bias")
+        nc.sync.dma_start(bias[:], b.rearrange("(h p) -> p h", p=P))
+
+        load_words(1)
+        for c0, n in GROUPS:
+            nc.sync.dma_start(x_raw[2][:, :, c0 : c0 + n], x_rows[2][:, :, c0 : c0 + n])
+
+        def interleave(copy, dst, raw):
+            copy(out=dst.rearrange("p (c i) t -> p c t i", i=4), in_=raw.rearrange("p t (c i) -> p c t i", i=4))
+
+        def quantize(codes, scales, grouped):
+            nc.vector.quantize_mx(
+                out=codes.bitcast(E4M3), scales=scales, in_=grouped.rearrange("p n t -> p (n t)")
+            )
+
+        vcopy = nc.vector.tensor_copy
+        scopy = nc.scalar.copy
+
+        u_grouped = keep.tile([P, U_PASSES, M, PACK], BF16, name="u_grouped", align_bytes=64)
+        u_codes = keep.tile([P, U_PASSES, M], U32, name="u_codes", align_bytes=64)
+        u_scales = keep.tile([P, U_PASSES, M], U8, name="u_scales", align_bytes=64)
+        for a, copy in enumerate((vcopy, scopy, vcopy)):
+            interleave(copy, u_grouped[:, a, :, :], u_raw[:, a, :, :])
+        for a in range(U_PASSES):
+            quantize(u_codes[:, a, :], u_scales[:, a, :], u_grouped[:, a, :, :])
+
+        x_grouped = [keep.tile([P, S, PACK], BF16, name="x_grouped%d" % a, align_bytes=64) for a in range(U_PASSES)]
+        x_codes = [keep.tile([P, S], U32, name="x_codes%d" % a, align_bytes=64) for a in range(U_PASSES)]
+        x_scales = [keep.tile([P, S], U8, name="x_scales%d" % a, align_bytes=64) for a in range(U_PASSES)]
+
+        def copy_x(a, c0, c1, copy):
+            interleave(copy, x_grouped[a][:, c0:c1, :], x_raw[a][:, :, c0:c1])
+
+        def quantize_x(a, c0, c1):
+            quantize(x_codes[a][:, c0:c1], x_scales[a][:, c0:c1], x_grouped[a][:, c0:c1, :])
+
+        banks = [
+            [psum.tile([P, n], F32, name="bank%d_%d" % (h, c0)) for c0, n in GROUPS] for h in range(HALVES)
+        ]
+        results = [keep.tile([P, HALVES, n], F32, name="result%d" % c0) for c0, n in GROUPS]
+
+        def mm(g, h, lhsT, lhsT_scale, rhs, rhs_scale, start, stop):
+            nc.tensor.matmul_mx(
+                out=banks[h][g][:], lhsT=lhsT, lhsT_scale=lhsT_scale, rhs=rhs, rhs_scale=rhs_scale,
+                start=start, stop=stop,
+            )
+
+        def mm_x(a, g, start=False, stop=False):
+            c0, n = GROUPS[g]
+            for h in range(HALVES):
+                m = slice(h * P, (h + 1) * P)
+                mm(g, h, u_codes[:, a, m].bitcast(E4M3), u_scales[:, a, m],
+                   x_codes[a][:, c0 : c0 + n].bitcast(E4M3), x_scales[a][:, c0 : c0 + n], start, stop)
+
+        gathered = [keep.tile([P, S], U32, name="gathered%d" % a, align_bytes=64) for a in range(W_PASSES)]
+        gathered_scales = keep.tile([P, S], U8, name="gathered_scales", align_bytes=64)
+        pass_scales = [gathered_scales, moved_scales]
+
+        def gather_words(a):
+            nc.vector.tensor_copy(out=gathered[a][:], in_=tab_words[a][:].bitcast(U32).indirect(offsets[:]))
+
+        def mm_w(a, g):
+            c0, n = GROUPS[g]
+            for h in range(HALVES):
+                m = slice(h * P, (h + 1) * P)
+                mm(g, h, w_words[:, a, 2 * h * P : 2 * (h + 1) * P].bitcast(E2M1), w_scales[:, a, m],
+                   gathered[a][:, c0 : c0 + n].bitcast(E4M3), pass_scales[a][:, c0 : c0 + n], False, False)
+
+        copy_x(0, 0, 768, scopy)
+        copy_x(0, 768, 1536, vcopy)
+        for c0, n in GROUPS:
+            quantize_x(0, c0, c0 + n)
+        for g in range(len(GROUPS)):
+            mm_x(0, g, start=True)
+
+        nc.vector.tensor_copy(out=gathered_scales[:], in_=tab_scales[:].indirect(offsets[:]))
+        for Q in range(4):
+            nc.gpsimd.dma_start(
+                moved_scales[32 * Q : 32 * Q + 4, :].bitcast(I32),
+                gathered_scales[32 * Q + 4 : 32 * Q + 32 : 8, :].bitcast(I32),
+            )
+        gather_words(0)
+        for g in range(len(GROUPS)):
+            mm_w(0, g)
+
+        copy_x(1, 0, 768, scopy)
+        copy_x(1, 768, 1536, vcopy)
+        for c0, n in GROUPS:
+            quantize_x(1, c0, c0 + n)
+        for g in range(len(GROUPS)):
+            mm_x(1, g)
+
+        gather_words(1)
+        for g in range(len(GROUPS)):
+            mm_w(1, g)
+
+        def finish(g):
+            c0, n = GROUPS[g]
+            mm_x(2, g, stop=True)
+            for h in range(HALVES):
+                nc.scalar.activation(out=results[g][:, h, :], in_=banks[h][g][:], func=SILU, bias=bias[:, h : h + 1])
+                nc.sync.dma_start(out[h * P : (h + 1) * P, c0 : c0 + n], results[g][:, h, :])
+
+        for g, (c0, n) in enumerate(GROUPS):
+            copy_x(2, c0, c0 + 192, scopy)
+            copy_x(2, c0 + 192, c0 + n, vcopy)
+            quantize_x(2, c0, c0 + n)
+            finish(g)

@@ -24,11 +24,14 @@ HALVES = M // P
 WORD_BYTES = K_PASS * T
 SCALE_ROWS = 16
 
-GROUPS = ((0, 512), (512, 512), (1024, 512))
+GROUPS = ((0, 512), (512, 512), (1024, 128), (1152, 128), (1280, 128), (1408, 128))
+SLICES = ((0, 512), (512, 512), (1024, 256), (1280, 256))
 
 
 def tile_list_tabx_silu_kernel(tc, tab, w4_words, w4_scales, x, u, b, offs, out):
     nc = tc.nc
+    vcopy = nc.vector.tensor_copy
+    scopy = nc.scalar.copy
     with ExitStack() as ctx:
         keep = ctx.enter_context(tc.tile_pool(name="keep", bufs=1))
         psum = ctx.enter_context(tc.psum_pool(name="psum", bufs=1))
@@ -36,13 +39,12 @@ def tile_list_tabx_silu_kernel(tc, tab, w4_words, w4_scales, x, u, b, offs, out)
         offsets = keep.tile([P, S // 16], U16, name="offsets")
         nc.sync.dma_start(offsets[:], offs)
 
+        tab_scales = keep.tile([P, T], U8, name="tab_scales", align_bytes=64)
+        nc.vector.memset(tab_scales[:].bitcast(I32), 0)
         act_in = keep.tile([P, 8], F32, name="act_in")
         act_out = keep.tile([P, 8], F32, name="act_out")
         nc.vector.memset(act_in[:], 0.0)
         nc.scalar.activation(out=act_out[:], in_=act_in[:], func=SILU)
-
-        tab_scales = keep.tile([P, T], U8, name="tab_scales", align_bytes=64)
-        nc.vector.memset(tab_scales[:].bitcast(I32), 0)
         w_scales = keep.tile([P, W_PASSES, M], U8, name="w_scales", align_bytes=64)
         nc.vector.memset(w_scales[:].rearrange("p a n -> p (a n)").bitcast(I32), 0)
         moved_scales = keep.tile([P, S], U8, name="moved_scales", align_bytes=64)
@@ -52,8 +54,16 @@ def tile_list_tabx_silu_kernel(tc, tab, w4_words, w4_scales, x, u, b, offs, out)
         nc.sync.dma_start(
             u_raw[:].rearrange("p a i n -> p a (i n)"), u.rearrange("(a p i) n -> p a (i n)", p=P, i=PACK)
         )
-        x_raw = [keep.tile([P, PACK, S], F32, name="x_raw%d" % a) for a in range(U_PASSES)]
+        scale_rows = tab[:, WORD_BYTES : WORD_BYTES + SCALE_ROWS * T].bitcast(I32)
+        rows0 = scale_rows[0].rearrange("(Q r t) -> r Q t", Q=4, r=4)
+        for r in range(4):
+            nc.sync.dma_start(tab_scales[r : P : 32, :].bitcast(I32), rows0[r])
+        nc.sync.dma_start(
+            tab_scales[4 : P : 8, :].bitcast(I32), scale_rows[1].rearrange("(q t) -> q t", q=SCALE_ROWS)
+        )
         x_rows = x.rearrange("(a p i) j -> a p i j", p=P, i=PACK)
+        x_raw = [keep.tile([P, PACK, S], F32, name="x_raw%d" % a) for a in range(2)]
+        x_last = [keep.tile([P, PACK, n], F32, name="x_last%d" % c0) for c0, n in SLICES]
         tab_words = [keep.tile([P, T], I32, name="tab_words%d" % a) for a in range(W_PASSES)]
 
         def load_words(a):
@@ -66,13 +76,6 @@ def tile_list_tabx_silu_kernel(tc, tab, w4_words, w4_scales, x, u, b, offs, out)
         nc.sync.dma_start(
             w_words[:].bitcast(I32), w4_words.bitcast(I32).rearrange("a p n -> p a n")
         )
-        scale_rows = tab[:, WORD_BYTES : WORD_BYTES + SCALE_ROWS * T].bitcast(I32)
-        rows0 = scale_rows[0].rearrange("(Q r t) -> r Q t", Q=4, r=4)
-        for r in range(4):
-            nc.sync.dma_start(tab_scales[r : P : 32, :].bitcast(I32), rows0[r])
-        nc.sync.dma_start(
-            tab_scales[4 : P : 8, :].bitcast(I32), scale_rows[1].rearrange("(q t) -> q t", q=SCALE_ROWS)
-        )
         load_words(0)
         nc.sync.dma_start(x_raw[1][:], x_rows[1])
         ws = w4_scales.bitcast(I32).rearrange("a (Q r) n -> r Q a n", r=4)
@@ -80,10 +83,9 @@ def tile_list_tabx_silu_kernel(tc, tab, w4_words, w4_scales, x, u, b, offs, out)
             nc.sync.dma_start(w_scales[r : P : 32, :, :].bitcast(I32), ws[r])
         bias = keep.tile([P, HALVES], F32, name="bias")
         nc.sync.dma_start(bias[:], b.rearrange("(h p) -> p h", p=P))
-
         load_words(1)
-        for c0, n in GROUPS:
-            nc.sync.dma_start(x_raw[2][:, :, c0 : c0 + n], x_rows[2][:, :, c0 : c0 + n])
+        for (c0, n), tile in zip(SLICES, x_last):
+            nc.sync.dma_start(tile[:], x_rows[2][:, :, c0 : c0 + n])
 
         def interleave(copy, dst, raw):
             copy(out=dst.rearrange("p (c i) t -> p c t i", i=4), in_=raw.rearrange("p t (c i) -> p c t i", i=4))
@@ -93,65 +95,78 @@ def tile_list_tabx_silu_kernel(tc, tab, w4_words, w4_scales, x, u, b, offs, out)
                 out=codes.bitcast(E4M3), scales=scales, in_=grouped.rearrange("p n t -> p (n t)")
             )
 
-        vcopy = nc.vector.tensor_copy
-        scopy = nc.scalar.copy
-
         u_grouped = keep.tile([P, U_PASSES, M, PACK], BF16, name="u_grouped", align_bytes=64)
         u_codes = keep.tile([P, U_PASSES, M], U32, name="u_codes", align_bytes=64)
         u_scales = keep.tile([P, U_PASSES, M], U8, name="u_scales", align_bytes=64)
-        for a, copy in enumerate((vcopy, scopy, vcopy)):
-            interleave(copy, u_grouped[:, a, :, :], u_raw[:, a, :, :])
-        for a in range(U_PASSES):
-            quantize(u_codes[:, a, :], u_scales[:, a, :], u_grouped[:, a, :, :])
-
         x_grouped = [keep.tile([P, S, PACK], BF16, name="x_grouped%d" % a, align_bytes=64) for a in range(U_PASSES)]
         x_codes = [keep.tile([P, S], U32, name="x_codes%d" % a, align_bytes=64) for a in range(U_PASSES)]
         x_scales = [keep.tile([P, S], U8, name="x_scales%d" % a, align_bytes=64) for a in range(U_PASSES)]
+        gathered = [keep.tile([P, S], U32, name="gathered%d" % a, align_bytes=64) for a in range(W_PASSES)]
+        gathered_scales = keep.tile([P, S], U8, name="gathered_scales", align_bytes=64)
+        pass_scales = [gathered_scales, moved_scales]
+        results = [keep.tile([P, HALVES, n], F32, name="result%d" % c0) for c0, n in SLICES]
 
         def copy_x(a, c0, c1, copy):
-            interleave(copy, x_grouped[a][:, c0:c1, :], x_raw[a][:, :, c0:c1])
+            if c1 > c0:
+                interleave(copy, x_grouped[a][:, c0:c1, :], x_raw[a][:, :, c0:c1])
 
-        def quantize_x(a, c0, c1):
-            quantize(x_codes[a][:, c0:c1], x_scales[a][:, c0:c1], x_grouped[a][:, c0:c1, :])
+        def copy_last(s, c0, c1, copy):
+            if c1 > c0:
+                first = SLICES[s][0]
+                interleave(copy, x_grouped[2][:, first + c0 : first + c1, :], x_last[s][:, :, c0:c1])
 
-        banks = [
-            [psum.tile([P, n], F32, name="bank%d_%d" % (h, c0)) for c0, n in GROUPS] for h in range(HALVES)
-        ]
-        results = [keep.tile([P, HALVES, n], F32, name="result%d" % c0) for c0, n in GROUPS]
+        def quantize_x(a, c0, n):
+            quantize(x_codes[a][:, c0 : c0 + n], x_scales[a][:, c0 : c0 + n], x_grouped[a][:, c0 : c0 + n, :])
 
-        def mm(g, h, lhsT, lhsT_scale, rhs, rhs_scale, start, stop):
-            nc.tensor.matmul_mx(
-                out=banks[h][g][:], lhsT=lhsT, lhsT_scale=lhsT_scale, rhs=rhs, rhs_scale=rhs_scale,
-                start=start, stop=stop,
-            )
+        tags = ("a", "b", "c", "d", "a", "b")
+        banks = {}
+
+        def open_group(g):
+            for h in range(HALVES):
+                banks[g, h] = psum.tile([P, GROUPS[g][1]], F32, name="bank%d_%d" % (g, h), tag="bank_%s%d" % (tags[g], h))
 
         def mm_x(a, g, start=False, stop=False):
             c0, n = GROUPS[g]
             for h in range(HALVES):
                 m = slice(h * P, (h + 1) * P)
-                mm(g, h, u_codes[:, a, m].bitcast(E4M3), u_scales[:, a, m],
-                   x_codes[a][:, c0 : c0 + n].bitcast(E4M3), x_scales[a][:, c0 : c0 + n], start, stop)
-
-        gathered = [keep.tile([P, S], U32, name="gathered%d" % a, align_bytes=64) for a in range(W_PASSES)]
-        gathered_scales = keep.tile([P, S], U8, name="gathered_scales", align_bytes=64)
-        pass_scales = [gathered_scales, moved_scales]
-
-        def gather_words(a):
-            nc.vector.tensor_copy(out=gathered[a][:], in_=tab_words[a][:].bitcast(U32).indirect(offsets[:]))
+                nc.tensor.matmul_mx(
+                    out=banks[g, h][:], lhsT=u_codes[:, a, m].bitcast(E4M3), lhsT_scale=u_scales[:, a, m],
+                    rhs=x_codes[a][:, c0 : c0 + n].bitcast(E4M3), rhs_scale=x_scales[a][:, c0 : c0 + n],
+                    start=start, stop=stop,
+                )
 
         def mm_w(a, g):
             c0, n = GROUPS[g]
             for h in range(HALVES):
                 m = slice(h * P, (h + 1) * P)
-                mm(g, h, w_words[:, a, 2 * h * P : 2 * (h + 1) * P].bitcast(E2M1), w_scales[:, a, m],
-                   gathered[a][:, c0 : c0 + n].bitcast(E4M3), pass_scales[a][:, c0 : c0 + n], False, False)
+                nc.tensor.matmul_mx(
+                    out=banks[g, h][:], lhsT=w_words[:, a, 2 * h * P : 2 * (h + 1) * P].bitcast(E2M1),
+                    lhsT_scale=w_scales[:, a, m],
+                    rhs=gathered[a][:, c0 : c0 + n].bitcast(E4M3), rhs_scale=pass_scales[a][:, c0 : c0 + n],
+                    start=False, stop=False,
+                )
 
-        copy_x(0, 0, 768, scopy)
-        copy_x(0, 768, 1536, vcopy)
-        for c0, n in GROUPS:
-            quantize_x(0, c0, c0 + n)
-        for g in range(len(GROUPS)):
-            mm_x(0, g, start=True)
+        def gather_words(a):
+            nc.vector.tensor_copy(out=gathered[a][:], in_=tab_words[a][:].bitcast(U32).indirect(offsets[:]))
+
+        def silu(s, g):
+            first = SLICES[s][0]
+            c0, n = GROUPS[g]
+            for h in range(HALVES):
+                nc.scalar.activation(
+                    out=results[s][:, h, c0 - first : c0 - first + n], in_=banks[g, h][:], func=SILU,
+                    bias=bias[:, h : h + 1],
+                )
+
+        def store(s):
+            c0, n = SLICES[s]
+            for h in range(HALVES):
+                nc.sync.dma_start(out[h * P : (h + 1) * P, c0 : c0 + n], results[s][:, h, :])
+
+        for a in range(U_PASSES):
+            interleave(scopy if a == 1 else vcopy, u_grouped[:, a, :, :], u_raw[:, a, :, :])
+        for a in range(U_PASSES):
+            quantize(u_codes[:, a, :], u_scales[:, a, :], u_grouped[:, a, :, :])
 
         nc.vector.tensor_copy(out=gathered_scales[:], in_=tab_scales[:].indirect(offsets[:]))
         for Q in range(4):
@@ -159,30 +174,51 @@ def tile_list_tabx_silu_kernel(tc, tab, w4_words, w4_scales, x, u, b, offs, out)
                 moved_scales[32 * Q : 32 * Q + 4, :].bitcast(I32),
                 gathered_scales[32 * Q + 4 : 32 * Q + 32 : 8, :].bitcast(I32),
             )
+
+        def x_pass(a, split):
+            copy_x(a, 0, 512, scopy)
+            copy_x(a, 1024, 1536, vcopy)
+            copy_x(a, 512, split, scopy)
+            copy_x(a, split, 1024, vcopy)
+            quantize_x(a, 1024, 512)
+            quantize_x(a, 0, 512)
+            quantize_x(a, 512, 512)
+
+        for g in range(4):
+            open_group(g)
+        x_pass(0, 896)
+        for g in (2, 3, 0, 1):
+            mm_x(0, g, start=True)
         gather_words(0)
-        for g in range(len(GROUPS)):
+        for g in range(4):
             mm_w(0, g)
-
-        copy_x(1, 0, 768, scopy)
-        copy_x(1, 768, 1536, vcopy)
-        for c0, n in GROUPS:
-            quantize_x(1, c0, c0 + n)
-        for g in range(len(GROUPS)):
+        x_pass(1, 896)
+        for g in (2, 3, 0, 1):
             mm_x(1, g)
-
         gather_words(1)
-        for g in range(len(GROUPS)):
+        for g in range(4):
             mm_w(1, g)
 
-        def finish(g):
-            c0, n = GROUPS[g]
-            mm_x(2, g, stop=True)
-            for h in range(HALVES):
-                nc.scalar.activation(out=results[g][:, h, :], in_=banks[h][g][:], func=SILU, bias=bias[:, h : h + 1])
-                nc.sync.dma_start(out[h * P : (h + 1) * P, c0 : c0 + n], results[g][:, h, :])
+        def early_passes(g):
+            open_group(g)
+            mm_x(0, g, start=True)
+            mm_w(0, g)
+            mm_x(1, g)
+            mm_w(1, g)
 
-        for g, (c0, n) in enumerate(GROUPS):
-            copy_x(2, c0, c0 + 192, scopy)
-            copy_x(2, c0 + 192, c0 + n, vcopy)
-            quantize_x(2, c0, c0 + n)
-            finish(g)
+        def last_pass(s, groups, split):
+            c0, n = SLICES[s]
+            copy_last(s, 0, split, scopy)
+            copy_last(s, split, n, vcopy)
+            quantize_x(2, c0, n)
+            for g in groups:
+                mm_x(2, g, stop=True)
+                silu(s, g)
+            store(s)
+
+        last_pass(0, (0,), 320)
+        last_pass(1, (1,), 128)
+        early_passes(4)
+        early_passes(5)
+        last_pass(2, (2, 3), 0)
+        last_pass(3, (4, 5), 0)

@@ -24,8 +24,8 @@ HALVES = M // P
 WORD_BYTES = K_PASS * T
 SCALE_ROWS = 16
 
-GROUPS = ((0, 512), (512, 512), (1024, 128), (1152, 128), (1280, 128), (1408, 128))
-SLICES = ((0, 512), (512, 512), (1024, 256), (1280, 256))
+GROUPS = ((0, 512), (512, 512), (1024, 512))
+SLICES = ((0, 512), (512, 512), (1024, 384), (1408, 128))
 
 
 def tile_list_tabx_silu_kernel(tc, tab, w4_words, w4_scales, x, u, b, offs, out):
@@ -62,6 +62,7 @@ def tile_list_tabx_silu_kernel(tc, tab, w4_words, w4_scales, x, u, b, offs, out)
             tab_scales[4 : P : 8, :].bitcast(I32), scale_rows[1].rearrange("(q t) -> q t", q=SCALE_ROWS)
         )
         x_rows = x.rearrange("(a p i) j -> a p i j", p=P, i=PACK)
+        x_runs = x.rearrange("(a p i) j -> a p (i j)", p=P, i=PACK)
         x_raw = [keep.tile([P, PACK, S], F32, name="x_raw%d" % a) for a in range(2)]
         x_last = [keep.tile([P, PACK, n], F32, name="x_last%d" % c0) for c0, n in SLICES]
         tab_words = [keep.tile([P, T], I32, name="tab_words%d" % a) for a in range(W_PASSES)]
@@ -71,13 +72,13 @@ def tile_list_tabx_silu_kernel(tc, tab, w4_words, w4_scales, x, u, b, offs, out)
                 tab_words[a][:], tab[a, 0:WORD_BYTES].rearrange("(p n) -> p n", p=P).bitcast(I32)
             )
 
-        nc.sync.dma_start(x_raw[0][:], x_rows[0])
+        nc.sync.dma_start(x_raw[0][:].rearrange("p i j -> p (i j)"), x_runs[0])
         w_words = keep.tile([P, W_PASSES, 2 * M], U8, name="w_words", align_bytes=64)
         nc.sync.dma_start(
             w_words[:].bitcast(I32), w4_words.bitcast(I32).rearrange("a p n -> p a n")
         )
         load_words(0)
-        nc.sync.dma_start(x_raw[1][:], x_rows[1])
+        nc.sync.dma_start(x_raw[1][:].rearrange("p i j -> p (i j)"), x_runs[1])
         ws = w4_scales.bitcast(I32).rearrange("a (Q r) n -> r Q a n", r=4)
         for r in range(4):
             nc.sync.dma_start(w_scales[r : P : 32, :, :].bitcast(I32), ws[r])
@@ -104,7 +105,7 @@ def tile_list_tabx_silu_kernel(tc, tab, w4_words, w4_scales, x, u, b, offs, out)
         gathered = [keep.tile([P, S], U32, name="gathered%d" % a, align_bytes=64) for a in range(W_PASSES)]
         gathered_scales = keep.tile([P, S], U8, name="gathered_scales", align_bytes=64)
         pass_scales = [gathered_scales, moved_scales]
-        results = [keep.tile([P, HALVES, n], F32, name="result%d" % c0) for c0, n in SLICES]
+        results = [keep.tile([P, n], F32, name="result%d_%d" % (c0, h)) for c0, n in GROUPS for h in range(HALVES)]
 
         def copy_x(a, c0, c1, copy):
             if c1 > c0:
@@ -118,19 +119,14 @@ def tile_list_tabx_silu_kernel(tc, tab, w4_words, w4_scales, x, u, b, offs, out)
         def quantize_x(a, c0, n):
             quantize(x_codes[a][:, c0 : c0 + n], x_scales[a][:, c0 : c0 + n], x_grouped[a][:, c0 : c0 + n, :])
 
-        tags = ("a", "b", "c", "d", "a", "b")
-        banks = {}
-
-        def open_group(g):
-            for h in range(HALVES):
-                banks[g, h] = psum.tile([P, GROUPS[g][1]], F32, name="bank%d_%d" % (g, h), tag="bank_%s%d" % (tags[g], h))
+        banks = [psum.tile([P, n], F32, name="bank%d_%d" % (c0, h)) for c0, n in GROUPS for h in range(HALVES)]
 
         def mm_x(a, g, start=False, stop=False):
             c0, n = GROUPS[g]
             for h in range(HALVES):
                 m = slice(h * P, (h + 1) * P)
                 nc.tensor.matmul_mx(
-                    out=banks[g, h][:], lhsT=u_codes[:, a, m].bitcast(E4M3), lhsT_scale=u_scales[:, a, m],
+                    out=banks[HALVES * g + h][:], lhsT=u_codes[:, a, m].bitcast(E4M3), lhsT_scale=u_scales[:, a, m],
                     rhs=x_codes[a][:, c0 : c0 + n].bitcast(E4M3), rhs_scale=x_scales[a][:, c0 : c0 + n],
                     start=start, stop=stop,
                 )
@@ -140,7 +136,7 @@ def tile_list_tabx_silu_kernel(tc, tab, w4_words, w4_scales, x, u, b, offs, out)
             for h in range(HALVES):
                 m = slice(h * P, (h + 1) * P)
                 nc.tensor.matmul_mx(
-                    out=banks[g, h][:], lhsT=w_words[:, a, 2 * h * P : 2 * (h + 1) * P].bitcast(E2M1),
+                    out=banks[HALVES * g + h][:], lhsT=w_words[:, a, 2 * h * P : 2 * (h + 1) * P].bitcast(E2M1),
                     lhsT_scale=w_scales[:, a, m],
                     rhs=gathered[a][:, c0 : c0 + n].bitcast(E4M3), rhs_scale=pass_scales[a][:, c0 : c0 + n],
                     start=False, stop=False,
@@ -149,19 +145,15 @@ def tile_list_tabx_silu_kernel(tc, tab, w4_words, w4_scales, x, u, b, offs, out)
         def gather_words(a):
             nc.vector.tensor_copy(out=gathered[a][:], in_=tab_words[a][:].bitcast(U32).indirect(offsets[:]))
 
-        def silu(s, g):
-            first = SLICES[s][0]
+        def finish(g):
             c0, n = GROUPS[g]
+            mm_x(2, g, stop=True)
             for h in range(HALVES):
+                result = results[HALVES * g + h]
                 nc.scalar.activation(
-                    out=results[s][:, h, c0 - first : c0 - first + n], in_=banks[g, h][:], func=SILU,
-                    bias=bias[:, h : h + 1],
+                    out=result[:], in_=banks[HALVES * g + h][:], func=SILU, bias=bias[:, h : h + 1]
                 )
-
-        def store(s):
-            c0, n = SLICES[s]
-            for h in range(HALVES):
-                nc.sync.dma_start(out[h * P : (h + 1) * P, c0 : c0 + n], results[s][:, h, :])
+                nc.sync.dma_start(out[h * P : (h + 1) * P, c0 : c0 + n], result[:])
 
         for a in range(U_PASSES):
             interleave(scopy if a == 1 else vcopy, u_grouped[:, a, :, :], u_raw[:, a, :, :])
@@ -184,41 +176,30 @@ def tile_list_tabx_silu_kernel(tc, tab, w4_words, w4_scales, x, u, b, offs, out)
             quantize_x(a, 0, 512)
             quantize_x(a, 512, 512)
 
-        for g in range(4):
-            open_group(g)
         x_pass(0, 896)
-        for g in (2, 3, 0, 1):
+        for g in (2, 0, 1):
             mm_x(0, g, start=True)
         gather_words(0)
-        for g in range(4):
+        for g in range(len(GROUPS)):
             mm_w(0, g)
         x_pass(1, 896)
-        for g in (2, 3, 0, 1):
+        for g in (2, 0, 1):
             mm_x(1, g)
         gather_words(1)
-        for g in range(4):
+        for g in range(len(GROUPS)):
             mm_w(1, g)
 
-        def early_passes(g):
-            open_group(g)
-            mm_x(0, g, start=True)
-            mm_w(0, g)
-            mm_x(1, g)
-            mm_w(1, g)
-
-        def last_pass(s, groups, split):
-            c0, n = SLICES[s]
-            copy_last(s, 0, split, scopy)
-            copy_last(s, split, n, vcopy)
-            quantize_x(2, c0, n)
-            for g in groups:
-                mm_x(2, g, stop=True)
-                silu(s, g)
-            store(s)
-
-        last_pass(0, (0,), 320)
-        last_pass(1, (1,), 128)
-        early_passes(4)
-        early_passes(5)
-        last_pass(2, (2, 3), 0)
-        last_pass(3, (4, 5), 0)
+        copy_last(0, 0, 320, scopy)
+        copy_last(0, 320, 512, vcopy)
+        quantize_x(2, 0, 512)
+        finish(0)
+        copy_last(1, 0, 128, scopy)
+        copy_last(1, 128, 512, vcopy)
+        quantize_x(2, 512, 512)
+        finish(1)
+        copy_last(2, 0, 384, vcopy)
+        quantize_x(2, 1024, 256)
+        quantize_x(2, 1280, 128)
+        copy_last(3, 0, 128, vcopy)
+        quantize_x(2, 1408, 128)
+        finish(2)

@@ -142,18 +142,22 @@ def tile_list_tabx_silu_kernel(tc, tab, w4_words, w4_scales, x, u, b, offs, out)
                     start=False, stop=False,
                 )
 
-        def gather_words(a):
-            nc.vector.tensor_copy(out=gathered[a][:], in_=tab_words[a][:].bitcast(U32).indirect(offsets[:]))
+        def gather_words(a, c0, c1):
+            nc.vector.tensor_copy(
+                out=gathered[a][:, c0:c1],
+                in_=tab_words[a][:].bitcast(U32).indirect(offsets[:, c0 // 16 : c1 // 16]),
+            )
 
-        def finish(g):
+        def finish(g, cuts):
             c0, n = GROUPS[g]
             mm_x(2, g, stop=True)
             for h in range(HALVES):
-                result = results[HALVES * g + h]
-                nc.scalar.activation(
-                    out=result[:], in_=banks[HALVES * g + h][:], func=SILU, bias=bias[:, h : h + 1]
-                )
-                nc.sync.dma_start(out[h * P : (h + 1) * P, c0 : c0 + n], result[:])
+                bank, result = banks[HALVES * g + h], results[HALVES * g + h]
+                for lo, hi in cuts[h]:
+                    nc.scalar.activation(
+                        out=result[:, lo:hi], in_=bank[:, lo:hi], func=SILU, bias=bias[:, h : h + 1]
+                    )
+                    nc.sync.dma_start(out[h * P : (h + 1) * P, c0 + lo : c0 + hi], result[:, lo:hi])
 
         for a in range(U_PASSES):
             interleave(scopy if a == 1 else vcopy, u_grouped[:, a, :, :], u_raw[:, a, :, :])
@@ -176,30 +180,34 @@ def tile_list_tabx_silu_kernel(tc, tab, w4_words, w4_scales, x, u, b, offs, out)
             quantize_x(a, 0, 512)
             quantize_x(a, 512, 512)
 
-        x_pass(0, 896)
+        x_pass(0, 768)
         for g in (2, 0, 1):
             mm_x(0, g, start=True)
-        gather_words(0)
+        gather_words(0, 0, S)
         for g in range(len(GROUPS)):
             mm_w(0, g)
-        x_pass(1, 896)
+        x_pass(1, 768)
         for g in (2, 0, 1):
             mm_x(1, g)
-        gather_words(1)
-        for g in range(len(GROUPS)):
+        gather_words(1, 0, 1024)
+        for g in range(2):
             mm_w(1, g)
 
-        copy_last(0, 0, 320, scopy)
-        copy_last(0, 320, 512, vcopy)
+        whole = ((0, 512),)
+        copy_last(0, 128, 512, scopy)
+        copy_last(0, 0, 128, vcopy)
+        copy_last(1, 288, 512, scopy)
+        copy_last(2, 320, 384, scopy)
         quantize_x(2, 0, 512)
-        finish(0)
-        copy_last(1, 0, 128, scopy)
-        copy_last(1, 128, 512, vcopy)
+        finish(0, (whole, whole))
+        gather_words(1, 1024, S)
+        mm_w(1, 2)
+        copy_last(1, 0, 288, vcopy)
         quantize_x(2, 512, 512)
-        finish(1)
-        copy_last(2, 0, 384, vcopy)
+        finish(1, (whole, whole))
+        copy_last(2, 0, 320, vcopy)
         quantize_x(2, 1024, 256)
         quantize_x(2, 1280, 128)
         copy_last(3, 0, 128, vcopy)
         quantize_x(2, 1408, 128)
-        finish(2)
+        finish(2, (whole, ((0, 256), (256, 512))))

from contextlib import ExitStack

import concourse.mybir as mybir

K, L, M, T, S = 1024, 1536, 256, 4096, 1536
FLOPS = 2 * M * S * (K + L)

F32 = mybir.dt.float32
BF16 = mybir.dt.bfloat16
I32 = mybir.dt.int32
U32 = mybir.dt.uint32
U16 = mybir.dt.uint16
U8 = mybir.dt.uint8
E4M3 = mybir.dt.float8_e4m3fn_x4
E2M1 = mybir.dt.float4_e2m1fn_x4
SILU = mybir.ActivationFunctionType.Silu

P = 128
PACK = 4
K_PASS = P * PACK
W_PASSES = K // K_PASS
U_PASSES = L // K_PASS
HALVES = M // P
WORD_BYTES = K_PASS * T
SCALE_ROWS = 16

GROUPS = ((0, 512), (512, 512), (1024, 512))
SLICES = ((0, 512), (512, 512), (1024, 384), (1408, 128))


def tile_list_tabx_silu_kernel(tc, tab, w4_words, w4_scales, x, u, b, offs, out):
    nc = tc.nc
    vcopy = nc.vector.tensor_copy
    scopy = nc.scalar.copy
    with ExitStack() as ctx:
        keep = ctx.enter_context(tc.tile_pool(name="keep", bufs=1))
        psum = ctx.enter_context(tc.psum_pool(name="psum", bufs=1))

        offsets = keep.tile([P, S // 16], U16, name="offsets")
        nc.sync.dma_start(offsets[:], offs)

        tab_scales = keep.tile([P, T], U8, name="tab_scales", align_bytes=64)
        nc.vector.memset(tab_scales[:].bitcast(I32), 0)
        act_in = keep.tile([P, 8], F32, name="act_in")
        act_out = keep.tile([P, 8], F32, name="act_out")
        nc.vector.memset(act_in[:], 0.0)
        nc.scalar.activation(out=act_out[:], in_=act_in[:], func=SILU)
        w_scales = keep.tile([P, W_PASSES, M], U8, name="w_scales", align_bytes=64)
        nc.vector.memset(w_scales[:].rearrange("p a n -> p (a n)").bitcast(I32), 0)
        moved_scales = keep.tile([P, S], U8, name="moved_scales", align_bytes=64)
        nc.vector.memset(moved_scales[:].bitcast(I32), 0)

        u_raw = keep.tile([P, U_PASSES, PACK, M], F32, name="u_raw")
        nc.sync.dma_start(
            u_raw[:].rearrange("p a i n -> p a (i n)"), u.rearrange("(a p i) n -> p a (i n)", p=P, i=PACK)
        )
        scale_rows = tab[:, WORD_BYTES : WORD_BYTES + SCALE_ROWS * T].bitcast(I32)
        rows0 = scale_rows[0].rearrange("(Q r t) -> r Q t", Q=4, r=4)
        for r in range(4):
            nc.sync.dma_start(tab_scales[r : P : 32, :].bitcast(I32), rows0[r])
        nc.sync.dma_start(
            tab_scales[4 : P : 8, :].bitcast(I32), scale_rows[1].rearrange("(q t) -> q t", q=SCALE_ROWS)
        )
        x_rows = x.rearrange("(a p i) j -> a p i j", p=P, i=PACK)
        x_runs = x.rearrange("(a p i) j -> a p (i j)", p=P, i=PACK)
        x_raw = [keep.tile([P, PACK, S], F32, name="x_raw%d" % a) for a in range(2)]
        x_last = [keep.tile([P, PACK, n], F32, name="x_last%d" % c0) for c0, n in SLICES]
        tab_words = [keep.tile([P, T], I32, name="tab_words%d" % a) for a in range(W_PASSES)]

        def load_words(a):
            nc.sync.dma_start(
                tab_words[a][:], tab[a, 0:WORD_BYTES].rearrange("(p n) -> p n", p=P).bitcast(I32)
            )

        nc.sync.dma_start(x_raw[0][:].rearrange("p i j -> p (i j)"), x_runs[0])
        w_words = keep.tile([P, W_PASSES, 2 * M], U8, name="w_words", align_bytes=64)
        nc.sync.dma_start(
            w_words[:].bitcast(I32), w4_words.bitcast(I32).rearrange("a p n -> p a n")
        )
        load_words(0)
        nc.sync.dma_start(x_raw[1][:].rearrange("p i j -> p (i j)"), x_runs[1])
        ws = w4_scales.bitcast(I32).rearrange("a (Q r) n -> r Q a n", r=4)
        for r in range(4):
            nc.sync.dma_start(w_scales[r : P : 32, :, :].bitcast(I32), ws[r])
        bias = keep.tile([P, HALVES], F32, name="bias")
        nc.sync.dma_start(bias[:], b.rearrange("(h p) -> p h", p=P))
        load_words(1)
        for (c0, n), tile in zip(SLICES, x_last):
            nc.sync.dma_start(tile[:], x_rows[2][:, :, c0 : c0 + n])

        def interleave(copy, dst, raw):
            copy(out=dst.rearrange("p (c i) t -> p c t i", i=4), in_=raw.rearrange("p t (c i) -> p c t i", i=4))

        def quantize(codes, scales, grouped):
            nc.vector.quantize_mx(
                out=codes.bitcast(E4M3), scales=scales, in_=grouped.rearrange("p n t -> p (n t)")
            )

        u_grouped = keep.tile([P, U_PASSES, M, PACK], BF16, name="u_grouped", align_bytes=64)
        u_codes = keep.tile([P, U_PASSES, M], U32, name="u_codes", align_bytes=64)
        u_scales = keep.tile([P, U_PASSES, M], U8, name="u_scales", align_bytes=64)
        x_grouped = [keep.tile([P, S, PACK], BF16, name="x_grouped%d" % a, align_bytes=64) for a in range(U_PASSES)]
        x_codes = [keep.tile([P, S], U32, name="x_codes%d" % a, align_bytes=64) for a in range(U_PASSES)]
        x_scales = [keep.tile([P, S], U8, name="x_scales%d" % a, align_bytes=64) for a in range(U_PASSES)]
        gathered = [keep.tile([P, S], U32, name="gathered%d" % a, align_bytes=64) for a in range(W_PASSES)]
        gathered_scales = keep.tile([P, S], U8, name="gathered_scales", align_bytes=64)
        pass_scales = [gathered_scales, moved_scales]
        results = [keep.tile([P, n], F32, name="result%d_%d" % (c0, h)) for c0, n in GROUPS for h in range(HALVES)]

        def copy_x(a, c0, c1, copy):
            if c1 > c0:
                interleave(copy, x_grouped[a][:, c0:c1, :], x_raw[a][:, :, c0:c1])

        def copy_last(s, c0, c1, copy):
            if c1 > c0:
                first = SLICES[s][0]
                interleave(copy, x_grouped[2][:, first + c0 : first + c1, :], x_last[s][:, :, c0:c1])

        def quantize_x(a, c0, n):
            quantize(x_codes[a][:, c0 : c0 + n], x_scales[a][:, c0 : c0 + n], x_grouped[a][:, c0 : c0 + n, :])

        banks = [psum.tile([P, n], F32, name="bank%d_%d" % (c0, h)) for c0, n in GROUPS for h in range(HALVES)]

        def mm_x(a, g, start=False, stop=False):
            c0, n = GROUPS[g]
            for h in range(HALVES):
                m = slice(h * P, (h + 1) * P)
                nc.tensor.matmul_mx(
                    out=banks[HALVES * g + h][:], lhsT=u_codes[:, a, m].bitcast(E4M3), lhsT_scale=u_scales[:, a, m],
                    rhs=x_codes[a][:, c0 : c0 + n].bitcast(E4M3), rhs_scale=x_scales[a][:, c0 : c0 + n],
                    start=start, stop=stop,
                )

        def mm_w(a, g):
            c0, n = GROUPS[g]
            for h in range(HALVES):
                m = slice(h * P, (h + 1) * P)
                nc.tensor.matmul_mx(
                    out=banks[HALVES * g + h][:], lhsT=w_words[:, a, 2 * h * P : 2 * (h + 1) * P].bitcast(E2M1),
                    lhsT_scale=w_scales[:, a, m],
                    rhs=gathered[a][:, c0 : c0 + n].bitcast(E4M3), rhs_scale=pass_scales[a][:, c0 : c0 + n],
                    start=False, stop=False,
                )

        def gather_words(a, c0, c1):
            nc.vector.tensor_copy(
                out=gathered[a][:, c0:c1],
                in_=tab_words[a][:].bitcast(U32).indirect(offsets[:, c0 // 16 : c1 // 16]),
            )

        def finish(g, cuts):
            c0, n = GROUPS[g]
            mm_x(2, g, stop=True)
            for h in range(HALVES):
                bank, result = banks[HALVES * g + h], results[HALVES * g + h]
                for lo, hi in cuts[h]:
                    nc.scalar.activation(
                        out=result[:, lo:hi], in_=bank[:, lo:hi], func=SILU, bias=bias[:, h : h + 1]
                    )
                    nc.sync.dma_start(out[h * P : (h + 1) * P, c0 + lo : c0 + hi], result[:, lo:hi])

        for a in range(U_PASSES):
            interleave(scopy if a == 1 else vcopy, u_grouped[:, a, :, :], u_raw[:, a, :, :])
        for a in range(U_PASSES):
            quantize(u_codes[:, a, :], u_scales[:, a, :], u_grouped[:, a, :, :])

        nc.vector.tensor_copy(out=gathered_scales[:], in_=tab_scales[:].indirect(offsets[:]))
        for Q in range(4):
            nc.gpsimd.dma_start(
                moved_scales[32 * Q : 32 * Q + 4, :].bitcast(I32),
                gathered_scales[32 * Q + 4 : 32 * Q + 32 : 8, :].bitcast(I32),
            )

        def x_pass(a, split):
            copy_x(a, 0, 512, scopy)
            copy_x(a, 1024, 1536, vcopy)
            copy_x(a, 512, split, scopy)
            copy_x(a, split, 1024, vcopy)
            quantize_x(a, 1024, 512)
            quantize_x(a, 0, 512)
            quantize_x(a, 512, 512)

        x_pass(0, 768)
        for g in (2, 0, 1):
            mm_x(0, g, start=True)
        gather_words(0, 0, S)
        for g in range(len(GROUPS)):
            mm_w(0, g)
        x_pass(1, 768)
        for g in (2, 0, 1):
            mm_x(1, g)
        gather_words(1, 0, 1024)
        for g in range(2):
            mm_w(1, g)

        whole = ((0, 512),)
        copy_last(0, 128, 512, scopy)
        copy_last(0, 0, 128, vcopy)
        copy_last(1, 288, 512, scopy)
        copy_last(2, 320, 384, scopy)
        quantize_x(2, 0, 512)
        finish(0, (whole, whole))
        gather_words(1, 1024, S)
        mm_w(1, 2)
        copy_last(1, 0, 288, vcopy)
        quantize_x(2, 512, 512)
        finish(1, (whole, whole))
        copy_last(2, 0, 320, vcopy)
        quantize_x(2, 1024, 256)
        quantize_x(2, 1280, 128)
        copy_last(3, 0, 128, vcopy)
        quantize_x(2, 1408, 128)
        finish(2, (whole, ((0, 256), (256, 512))))
